import numpy as np
import ml_dtypes


def mxq(x, axis, fmt="e4m3"):
    dtype, down = {"e4m3": (ml_dtypes.float8_e4m3fn, 7), "e5m2": (ml_dtypes.float8_e5m2, 14)}[fmt]
    v = np.moveaxis(np.asarray(x, np.float32).astype(ml_dtypes.bfloat16).astype(np.float64), axis, -1)
    blocks = v.reshape(v.shape[:-1] + (-1, 32))
    amax = np.abs(blocks).max(-1, keepdims=True)
    byte = np.maximum(np.where(amax > 0, np.frexp(amax)[1] - 1 + 127, 0) - down, 1)
    scale = np.exp2(byte - 127.0)
    codes = (blocks / scale).astype(np.float32).astype(dtype).astype(np.float64)
    return np.moveaxis((codes * scale).reshape(v.shape), -1, axis)


WIDE = False


def mx_kscale(k):
    if not WIDE:
        return np.ones(k)
    levels = np.array([10, -10, 5, -5, 0])
    if k % 512:
        return np.exp2(np.random.permutation(np.resize(levels, k // 32))).repeat(32)
    a = np.empty((k // 512, 16))
    for p in range(k // 512):
        a[p, :8] = np.random.permutation(np.resize(levels, 8))
        for g in range(8):
            far = levels[np.abs(levels - a[p, g]) >= 10]
            a[p, g + 8] = far[np.random.randint(len(far))]
    return np.exp2(a.ravel()).repeat(32)


def f64(x):
    return np.asarray(x).astype(np.float64)


def striped(idx):
    return np.tile(np.asarray(idx).reshape(-1, 16).T, (8, 1)).astype(np.uint16)


def unstriped(offs):
    return offs[:16].T.reshape(-1).astype(np.int64)


E2M1 = np.array([0.0, 0.5, 1.0, 1.5, 2.0, 3.0, 4.0, 6.0, -0.0, -0.5, -1.0, -1.5, -2.0, -3.0, -4.0, -6.0])


def pack_weight(w, fmt):
    k, n = w.shape
    w = f64(np.asarray(w, np.float32).astype(ml_dtypes.bfloat16)).reshape(k // 32, 32, n)
    amax = np.abs(w).max(1)
    if fmt == "e4m3":
        byte = np.frexp(amax)[1] - 1 + 127 - 7
    else:
        mant, ex = np.frexp(amax / 6.0)
        byte = np.where(mant > 0.5, ex, ex - 1) + 127
    byte = np.clip(np.where(amax > 0, byte, 1), 1, 254)
    scaled = (w * np.exp2(127.0 - byte)[:, None, :]).reshape(k, n).astype(np.float32)
    by_word = np.ascontiguousarray(scaled.reshape(k // 512, 128, 4, n).transpose(0, 1, 3, 2))
    if fmt == "e4m3":
        words = by_word.astype(ml_dtypes.float8_e4m3fn).view(np.uint8)
    else:
        c = by_word.astype(ml_dtypes.float4_e2m1fn).view(np.uint8) & 0xF
        words = (c[..., 0::2] | (c[..., 1::2] << 4)).reshape(k // 512, 128, 2 * n)
    return np.ascontiguousarray(words), np.ascontiguousarray(byte.astype(np.uint8).reshape(k // 512, 16, n))


def unpack_weight(words, scales, fmt):
    g, _, n = scales.shape
    words = np.ascontiguousarray(words).reshape(g, 128, n, -1)
    if fmt == "e4m3":
        vals = words.view(ml_dtypes.float8_e4m3fn).astype(np.float64)
    else:
        nib = np.empty((g, 128, n, 4), np.uint8)
        nib[..., 0::2] = words & 0xF
        nib[..., 1::2] = words >> 4
        vals = E2M1[nib]
    vals = vals * np.repeat(np.exp2(scales.astype(np.float64) - 127.0), 8, axis=1)[..., None]
    return vals.transpose(0, 1, 3, 2).reshape(g * 512, n)


K, T, V, J, L, N = 512, 1024, 512, 512, 512, 512


def setup_inputs():
    n = np.random.standard_normal
    idx = np.random.permutation(T)[:J]
    idx2 = np.random.randint(0, V, J)
    fk = mx_kscale(K)
    fl = mx_kscale(L)
    wap = pack_weight(n((K, N)) * 1 / np.sqrt(K) * fk[:, None], "e2m1")
    xsp = pack_weight(n((L, T)) / fl[:, None], "e4m3")
    wsp = pack_weight(n((L, N)) * 1 / np.sqrt(L) * fl[:, None], "e2m1")
    return {
        "xf": (n((K, T))).astype(np.float32),
        "cx": (n((K, V))).astype(np.float32),
        "fk": (np.random.uniform(0.5, 2.0, (K, 1)) / fk[:, None]).astype(np.float32),
        "wa_words": wap[0],
        "wa_scales": wap[1],
        "xs_words": xsp[0],
        "xs_scales": xsp[1],
        "ws_words": wsp[0],
        "ws_scales": wsp[1],
        "offs": striped(idx),
        "offs2": striped(idx2),
    }


def reference(xf, cx, fk, wa_words, wa_scales, xs_words, xs_scales, ws_words, ws_scales, offs, offs2):
    idx = unstriped(offs)
    idx2 = unstriped(offs2)
    wau = unpack_weight(wa_words, wa_scales, "e2m1")
    xsu = unpack_weight(xs_words, xs_scales, "e4m3")
    wsu = unpack_weight(ws_words, ws_scales, "e2m1")
    u = (f64(xf)[:, idx] + f64(cx)[:, idx2]) * f64(fk)
    uq = mxq(u, 0, "e4m3")
    p = wau.T @ uq
    d = np.maximum(p, 0.0)
    dp = np.zeros((N, T))
    dp[:, idx] = d
    z = wsu.T @ xsu
    y = z + dp
    return y

@@ -1,0 +1,144 @@
+from contextlib import ExitStack
+
+import concourse.mybir as mybir
+
+K, T, V, J, L, N = 512, 1024, 512, 512, 512, 512
+FLOPS = 2 * K * N * J + 2 * L * N * T
+
+F32 = mybir.dt.float32
+BF16 = mybir.dt.bfloat16
+I32 = mybir.dt.int32
+U32 = mybir.dt.uint32
+U16 = mybir.dt.uint16
+U8 = mybir.dt.uint8
+FP8X4 = mybir.dt.float8_e4m3fn_x4
+FP4X4 = mybir.dt.float4_e2m1fn_x4
+ADD = mybir.AluOpType.add
+COPY = mybir.ActivationFunctionType.Copy
+RELU = mybir.ActivationFunctionType.Relu
+
+P = 128
+PACK = 4
+HALF = J // 2
+BANK = 512
+BLOCKS = N // P
+
+
+def tile_moe_expert_reads_token_and_context_kernel(
+    tc, xf, cx, fk, wa_words, wa_scales, xs_words, xs_scales, ws_words, ws_scales, offs, offs2, out
+):
+    nc = tc.nc
+    with ExitStack() as ctx:
+        keep = ctx.enter_context(tc.tile_pool(name="keep", bufs=1))
+        psum = ctx.enter_context(tc.psum_pool(name="psum", bufs=1))
+
+        tok_list = keep.tile([P, J // 16], U16, name="tok_list")
+        ctx_list = keep.tile([P, J // 16], U16, name="ctx_list")
+        factor = keep.tile([P, PACK], F32, name="factor")
+        tokens = [keep.tile([P, T], F32, name="tokens%d" % t) for t in range(PACK)]
+        contexts = [keep.tile([P, V], F32, name="contexts%d" % t) for t in range(PACK)]
+        wa_w = keep.tile([P, 2 * N], U8, name="wa_w", align_bytes=64)
+        ws_w = keep.tile([P, 2 * N], U8, name="ws_w", align_bytes=64)
+        xs_w = keep.tile([P, T], U32, name="xs_w", align_bytes=64)
+        wa_s = keep.tile([P, N], U8, name="wa_s", align_bytes=64)
+        ws_s = keep.tile([P, N], U8, name="ws_s", align_bytes=64)
+        xs_s = keep.tile([P, T], U8, name="xs_s", align_bytes=64)
+        placed = [keep.tile([P, T], F32, name="placed%d" % b) for b in range(BLOCKS)]
+
+        for plane in (wa_s, ws_s, xs_s):
+            nc.gpsimd.memset(plane[:].bitcast(I32), 0)
+        for b in range(BLOCKS):
+            nc.vector.memset(placed[b][:], 0.0)
+
+        xf_rows = xf.rearrange("(p t) c -> t p c", t=PACK)
+        cx_rows = cx.rearrange("(p t) c -> t p c", t=PACK)
+        nc.sync.dma_start(ctx_list[:], offs2)
+        nc.sync.dma_start(contexts[0][:], cx_rows[0])
+        nc.sync.dma_start(tok_list[:], offs)
+        nc.sync.dma_start(tokens[0][:], xf_rows[0])
+        nc.sync.dma_start(factor[:], fk.rearrange("(p t) o -> p (t o)", t=PACK))
+        for t in range(1, PACK):
+            nc.sync.dma_start(contexts[t][:], cx_rows[t])
+            nc.sync.dma_start(tokens[t][:], xf_rows[t])
+
+        def load_scales(plane, rows):
+            for q in range(4):
+                nc.sync.dma_start(
+                    plane[32 * q : 32 * q + 4, :].bitcast(I32), rows[0, 4 * q : 4 * q + 4, :].bitcast(I32)
+                )
+
+        nc.sync.dma_start(wa_w[:].bitcast(I32), wa_words[0].bitcast(I32))
+        load_scales(wa_s, wa_scales)
+        nc.sync.dma_start(ws_w[:].bitcast(I32), ws_words[0].bitcast(I32))
+        nc.sync.dma_start(xs_w[:].bitcast(I32), xs_words[0].rearrange("p c r -> p (c r)").bitcast(I32))
+        load_scales(ws_s, ws_scales)
+        load_scales(xs_s, xs_scales)
+
+        def entries(lst, h):
+            return lst[:, h * HALF // 16 : (h + 1) * HALF // 16]
+
+        u = [keep.tile([P, HALF, PACK], BF16, name="u%d" % h, align_bytes=64) for h in range(2)]
+        for t in range(PACK):
+            for h in range(2):
+                picked = keep.tile([P, HALF], F32, name="picked%d%d" % (t, h))
+                summed = keep.tile([P, HALF], F32, name="summed%d%d" % (t, h))
+                nc.vector.tensor_copy(picked[:], contexts[t][:].indirect(entries(ctx_list, h)))
+                nc.vector.tensor_tensor(summed[:], tokens[t][:].indirect(entries(tok_list, h)), picked[:], ADD)
+                nc.scalar.activation(u[h][:, :, t], summed[:], COPY, scale=factor[:, t : t + 1])
+
+        d = [keep.tile([P, J], F32, name="d%d" % b) for b in range(BLOCKS)]
+        for h in range(2):
+            codes = keep.tile([P, HALF], U32, name="codes%d" % h, align_bytes=64)
+            scales = keep.tile([P, HALF], U8, name="scales%d" % h, align_bytes=64)
+            nc.vector.quantize_mx(
+                out=codes[:].bitcast(FP8X4), scales=scales[:], in_=u[h][:].rearrange("p j t -> p (j t)")
+            )
+            for b in range(BLOCKS):
+                acc = psum.tile([P, HALF], F32, name="expert_acc", tag="expert%d" % b)
+                nc.tensor.matmul_mx(
+                    out=acc[:],
+                    lhsT=wa_w[:, 2 * P * b : 2 * P * (b + 1)].bitcast(FP4X4),
+                    lhsT_scale=wa_s[:, P * b : P * (b + 1)],
+                    rhs=codes[:].bitcast(FP8X4),
+                    rhs_scale=scales[:],
+                    start=True,
+                    stop=True,
+                )
+                nc.scalar.activation(d[b][:, h * HALF : (h + 1) * HALF], acc[:], RELU)
+
+        def scatter(b, h):
+            if h is None:
+                nc.vector.tensor_copy(placed[b][:].indirect(tok_list[:]), d[b][:])
+            else:
+                nc.vector.tensor_copy(
+                    placed[b][:].indirect(entries(tok_list, h)), d[b][:, h * HALF : (h + 1) * HALF]
+                )
+
+        def finish(b):
+            for c in range(T // BANK):
+                cols = slice(c * BANK, (c + 1) * BANK)
+                z = psum.tile([P, BANK], F32, name="z", tag="shared%d%d" % (b % 2, c))
+                nc.tensor.matmul_mx(
+                    out=z[:],
+                    lhsT=ws_w[:, 2 * P * b : 2 * P * (b + 1)].bitcast(FP4X4),
+                    lhsT_scale=ws_s[:, P * b : P * (b + 1)],
+                    rhs=xs_w[:, cols].bitcast(FP8X4),
+                    rhs_scale=xs_s[:, cols],
+                    start=True,
+                    stop=True,
+                )
+                y = keep.tile([P, BANK], F32, name="y%d%d" % (b, c))
+                nc.vector.tensor_tensor(y[:], z[:], placed[b][:, cols], ADD)
+                nc.sync.dma_start(out[b * P : (b + 1) * P, cols], y[:])
+
+        scatter(0, 0)
+        scatter(1, 0)
+        scatter(0, 1)
+        scatter(1, 1)
+        finish(0)
+        scatter(2, None)
+        finish(1)
+        scatter(3, 0)
+        finish(2)
+        scatter(3, 1)
+        finish(3)

@@ -36,7 +36,8 @@ def tile_moe_expert_reads_token_and_context_kernel(
         ctx_list = keep.tile([P, J // 16], U16, name="ctx_list")
         factor = keep.tile([P, PACK], F32, name="factor")
         tokens = [keep.tile([P, T], F32, name="tokens%d" % t) for t in range(PACK)]
-        contexts = [keep.tile([P, V], F32, name="contexts%d" % t) for t in range(PACK)]
+        ctx_tiles = [keep.tile([P, 2 * V], F32, name="contexts%d" % t) for t in range(2)]
+        contexts = [ctx_tiles[t // 2][:, (t % 2) * V : (t % 2 + 1) * V] for t in range(PACK)]
         wa_w = keep.tile([P, 2 * N], U8, name="wa_w", align_bytes=64)
         ws_w = keep.tile([P, 2 * N], U8, name="ws_w", align_bytes=64)
         xs_w = keep.tile([P, T], U32, name="xs_w", align_bytes=64)
@@ -48,18 +49,21 @@ def tile_moe_expert_reads_token_and_context_kernel(
         for plane in (wa_s, ws_s, xs_s):
             nc.gpsimd.memset(plane[:].bitcast(I32), 0)
         for b in range(BLOCKS):
-            nc.vector.memset(placed[b][:], 0.0)
+            engine = nc.vector if b < 2 else nc.gpsimd
+            engine.memset(placed[b][:], 0.0)
 
         xf_rows = xf.rearrange("(p t) c -> t p c", t=PACK)
         cx_rows = cx.rearrange("(p t) c -> t p c", t=PACK)
         nc.sync.dma_start(ctx_list[:], offs2)
-        nc.sync.dma_start(contexts[0][:], cx_rows[0])
+        nc.scalar.dma_start(contexts[0], cx_rows[0])
         nc.sync.dma_start(tok_list[:], offs)
         nc.sync.dma_start(tokens[0][:], xf_rows[0])
         nc.sync.dma_start(factor[:], fk.rearrange("(p t) o -> p (t o)", t=PACK))
-        for t in range(1, PACK):
-            nc.sync.dma_start(contexts[t][:], cx_rows[t])
+        for t in range(1, PACK - 1):
+            nc.sync.dma_start(contexts[t], cx_rows[t])
             nc.sync.dma_start(tokens[t][:], xf_rows[t])
+        nc.sync.dma_start(tokens[3][:], xf_rows[3])
+        nc.sync.dma_start(contexts[3], cx_rows[3])
 
         def load_scales(plane, rows):
             for q in range(4):
@@ -74,50 +78,53 @@ def tile_moe_expert_reads_token_and_context_kernel(
         load_scales(ws_s, ws_scales)
         load_scales(xs_s, xs_scales)
 
+        def slots(h):
+            return slice(0, J) if h is None else slice(h * HALF, (h + 1) * HALF)
+
         def entries(lst, h):
-            return lst[:, h * HALF // 16 : (h + 1) * HALF // 16]
+            return lst[:, slots(h).start // 16 : slots(h).stop // 16]
 
-        u = [keep.tile([P, HALF, PACK], BF16, name="u%d" % h, align_bytes=64) for h in range(2)]
-        for t in range(PACK):
-            for h in range(2):
-                picked = keep.tile([P, HALF], F32, name="picked%d%d" % (t, h))
-                summed = keep.tile([P, HALF], F32, name="summed%d%d" % (t, h))
-                nc.vector.tensor_copy(picked[:], contexts[t][:].indirect(entries(ctx_list, h)))
-                nc.vector.tensor_tensor(summed[:], tokens[t][:].indirect(entries(tok_list, h)), picked[:], ADD)
-                nc.scalar.activation(u[h][:, :, t], summed[:], COPY, scale=factor[:, t : t + 1])
+        u = [keep.tile([P, HALF, PACK], BF16, name="u%d" % h, tag="u%d" % h, align_bytes=64) for h in range(2)]
+        codes = keep.tile([P, J], U32, name="codes", align_bytes=64)
+        scales = keep.tile([P, J], U8, name="scales", align_bytes=64)
 
-        d = [keep.tile([P, J], F32, name="d%d" % b) for b in range(BLOCKS)]
-        for h in range(2):
-            codes = keep.tile([P, HALF], U32, name="codes%d" % h, align_bytes=64)
-            scales = keep.tile([P, HALF], U8, name="scales%d" % h, align_bytes=64)
+        def gather(t, h):
+            window = ctx_tiles[1][:] if (t, h) == (2, 1) else contexts[t]
+            tag = "u0" if (t, h) == (3, 1) else "summed%d%d" % (t, h)
+            picked = keep.tile([P, HALF], F32, name="picked%d%d" % (t, h))
+            summed = keep.tile([P, HALF], F32, name="summed", tag=tag, align_bytes=64)
+            nc.vector.tensor_copy(picked[:], window.indirect(entries(ctx_list, h)))
+            nc.vector.tensor_tensor(summed[:], tokens[t][:].indirect(entries(tok_list, h)), picked[:], ADD)
+            nc.scalar.activation(u[h][:, :, t], summed[:], COPY, scale=factor[:, t : t + 1])
+
+        def quantise(h):
             nc.vector.quantize_mx(
-                out=codes[:].bitcast(FP8X4), scales=scales[:], in_=u[h][:].rearrange("p j t -> p (j t)")
+                out=codes[:, slots(h)].bitcast(FP8X4),
+                scales=scales[:, slots(h)],
+                in_=u[h][:].rearrange("p j t -> p (j t)"),
             )
-            for b in range(BLOCKS):
-                acc = psum.tile([P, HALF], F32, name="expert_acc", tag="expert%d" % b)
-                nc.tensor.matmul_mx(
-                    out=acc[:],
-                    lhsT=wa_w[:, 2 * P * b : 2 * P * (b + 1)].bitcast(FP4X4),
-                    lhsT_scale=wa_s[:, P * b : P * (b + 1)],
-                    rhs=codes[:].bitcast(FP8X4),
-                    rhs_scale=scales[:],
-                    start=True,
-                    stop=True,
-                )
-                nc.scalar.activation(d[b][:, h * HALF : (h + 1) * HALF], acc[:], RELU)
 
-        def scatter(b, h):
-            if h is None:
-                nc.vector.tensor_copy(placed[b][:].indirect(tok_list[:]), d[b][:])
-            else:
-                nc.vector.tensor_copy(
-                    placed[b][:].indirect(entries(tok_list, h)), d[b][:, h * HALF : (h + 1) * HALF]
-                )
+        def expert(b, h, bank):
+            width = slots(h).stop - slots(h).start
+            acc = psum.tile([P, width], F32, name="expert_acc", tag="bank%d" % bank)
+            nc.tensor.matmul_mx(
+                out=acc[:],
+                lhsT=wa_w[:, 2 * P * b : 2 * P * (b + 1)].bitcast(FP4X4),
+                lhsT_scale=wa_s[:, P * b : P * (b + 1)],
+                rhs=codes[:, slots(h)].bitcast(FP8X4),
+                rhs_scale=scales[:, slots(h)],
+                start=True,
+                stop=True,
+            )
+            tag = "u0" if (b, h) == (1, 0) else "d%d%s" % (b, h)
+            d = keep.tile([P, width], F32, name="d", tag=tag, align_bytes=64)
+            nc.scalar.activation(d[:], acc[:], RELU)
+            nc.vector.tensor_copy(placed[b][:].indirect(entries(tok_list, h)), d[:])
 
-        def finish(b):
+        def finish(b, banks):
             for c in range(T // BANK):
                 cols = slice(c * BANK, (c + 1) * BANK)
-                z = psum.tile([P, BANK], F32, name="z", tag="shared%d%d" % (b % 2, c))
+                z = psum.tile([P, BANK], F32, name="z", tag="bank%d" % banks[c])
                 nc.tensor.matmul_mx(
                     out=z[:],
                     lhsT=ws_w[:, 2 * P * b : 2 * P * (b + 1)].bitcast(FP4X4),
@@ -128,17 +135,26 @@ def tile_moe_expert_reads_token_and_context_kernel(
                     stop=True,
                 )
                 y = keep.tile([P, BANK], F32, name="y%d%d" % (b, c))
-                nc.vector.tensor_tensor(y[:], z[:], placed[b][:, cols], ADD)
+                if b == BLOCKS - 1:
+                    nc.vector.tensor_tensor(y[:], z[:], placed[b][:, cols], ADD)
+                else:
+                    zs = keep.tile([P, BANK], F32, name="zs%d%d" % (b, c))
+                    nc.scalar.copy(zs[:], z[:])
+                    nc.gpsimd.tensor_tensor(y[:], zs[:], placed[b][:, cols], ADD)
                 nc.sync.dma_start(out[b * P : (b + 1) * P, cols], y[:])
 
-        scatter(0, 0)
-        scatter(1, 0)
-        scatter(0, 1)
-        scatter(1, 1)
-        finish(0)
-        scatter(2, None)
-        finish(1)
-        scatter(3, 0)
-        finish(2)
-        scatter(3, 1)
-        finish(3)
+        for t, h in ((0, 0), (0, 1), (1, 0), (1, 1), (2, 0), (3, 0), (2, 1)):
+            gather(t, h)
+        quantise(0)
+        gather(3, 1)
+        expert(0, 0, 0)
+        quantise(1)
+        expert(1, 0, 1)
+        expert(0, 1, 2)
+        expert(1, 1, 3)
+        expert(2, None, 4)
+        expert(3, None, 5)
+        finish(0, (2, 3))
+        finish(1, (4, 5))
+        finish(2, (2, 3))
+        finish(3, (6, 7))

@@ -36,34 +36,30 @@ def tile_moe_expert_reads_token_and_context_kernel(
         ctx_list = keep.tile([P, J // 16], U16, name="ctx_list")
         factor = keep.tile([P, PACK], F32, name="factor")
         tokens = [keep.tile([P, T], F32, name="tokens%d" % t) for t in range(PACK)]
-        ctx_tiles = [keep.tile([P, 2 * V], F32, name="contexts%d" % t) for t in range(2)]
-        contexts = [ctx_tiles[t // 2][:, (t % 2) * V : (t % 2 + 1) * V] for t in range(PACK)]
+        contexts = [keep.tile([P, V], F32, name="contexts%d" % t) for t in range(PACK)]
         wa_w = keep.tile([P, 2 * N], U8, name="wa_w", align_bytes=64)
         ws_w = keep.tile([P, 2 * N], U8, name="ws_w", align_bytes=64)
         xs_w = keep.tile([P, T], U32, name="xs_w", align_bytes=64)
         wa_s = keep.tile([P, N], U8, name="wa_s", align_bytes=64)
         ws_s = keep.tile([P, N], U8, name="ws_s", align_bytes=64)
         xs_s = keep.tile([P, T], U8, name="xs_s", align_bytes=64)
-        placed = [keep.tile([P, T], F32, name="placed%d" % b) for b in range(BLOCKS)]
+        placed = {b: keep.tile([P, T], F32, name="placed%d" % b) for b in (0, 1, 3)}
 
         for plane in (wa_s, ws_s, xs_s):
             nc.gpsimd.memset(plane[:].bitcast(I32), 0)
-        for b in range(BLOCKS):
-            engine = nc.vector if b < 2 else nc.gpsimd
-            engine.memset(placed[b][:], 0.0)
+        for b in (0, 1, 3):
+            nc.vector.memset(placed[b][:].bitcast(I32), 0)
 
         xf_rows = xf.rearrange("(p t) c -> t p c", t=PACK)
         cx_rows = cx.rearrange("(p t) c -> t p c", t=PACK)
         nc.sync.dma_start(ctx_list[:], offs2)
-        nc.scalar.dma_start(contexts[0], cx_rows[0])
+        nc.sync.dma_start(contexts[0][:], cx_rows[0])
         nc.sync.dma_start(tok_list[:], offs)
         nc.sync.dma_start(tokens[0][:], xf_rows[0])
         nc.sync.dma_start(factor[:], fk.rearrange("(p t) o -> p (t o)", t=PACK))
-        for t in range(1, PACK - 1):
-            nc.sync.dma_start(contexts[t], cx_rows[t])
+        for t in range(1, PACK):
+            nc.sync.dma_start(contexts[t][:], cx_rows[t])
             nc.sync.dma_start(tokens[t][:], xf_rows[t])
-        nc.sync.dma_start(tokens[3][:], xf_rows[3])
-        nc.sync.dma_start(contexts[3], cx_rows[3])
 
         def load_scales(plane, rows):
             for q in range(4):
@@ -89,11 +85,9 @@ def tile_moe_expert_reads_token_and_context_kernel(
         scales = keep.tile([P, J], U8, name="scales", align_bytes=64)
 
         def gather(t, h):
-            window = ctx_tiles[1][:] if (t, h) == (2, 1) else contexts[t]
-            tag = "u0" if (t, h) == (3, 1) else "summed%d%d" % (t, h)
-            picked = keep.tile([P, HALF], F32, name="picked%d%d" % (t, h))
-            summed = keep.tile([P, HALF], F32, name="summed", tag=tag, align_bytes=64)
-            nc.vector.tensor_copy(picked[:], window.indirect(entries(ctx_list, h)))
+            picked = keep.tile([P, HALF], F32, name="picked", tag="picked%d%d" % (t, h))
+            summed = keep.tile([P, HALF], F32, name="summed%d%d" % (t, h))
+            nc.vector.tensor_copy(picked[:], contexts[t][:].indirect(entries(ctx_list, h)))
             nc.vector.tensor_tensor(summed[:], tokens[t][:].indirect(entries(tok_list, h)), picked[:], ADD)
             nc.scalar.activation(u[h][:, :, t], summed[:], COPY, scale=factor[:, t : t + 1])
 
@@ -104,36 +98,41 @@ def tile_moe_expert_reads_token_and_context_kernel(
                 in_=u[h][:].rearrange("p j t -> p (j t)"),
             )
 
-        def expert(b, h, bank):
-            width = slots(h).stop - slots(h).start
-            acc = psum.tile([P, width], F32, name="expert_acc", tag="bank%d" % bank)
+        def expert(b, lo, hi, bank):
+            acc = psum.tile([P, hi - lo], F32, name="expert_acc", tag="bank%d" % bank)
+            cuts = (lo, HALF, hi) if 0 < lo < HALF < hi else (lo, hi)
+            for first, last in zip(cuts, cuts[1:]):
+                nc.tensor.matmul_mx(
+                    out=acc[:, first - lo : last - lo],
+                    lhsT=wa_w[:, 2 * P * b : 2 * P * (b + 1)].bitcast(FP4X4),
+                    lhsT_scale=wa_s[:, P * b : P * (b + 1)],
+                    rhs=codes[:, first:last].bitcast(FP8X4),
+                    rhs_scale=scales[:, first:last],
+                    start=True,
+                    stop=True,
+                )
+            d = keep.tile([P, hi - lo], F32, name="d%d_%d" % (b, lo))
+            nc.scalar.activation(d[:], acc[:], RELU)
+            nc.vector.tensor_copy(placed[b][:].indirect(tok_list[:, lo // 16 : hi // 16]), d[:])
+
+        def shared(b, c, bank):
+            cols = slice(c * BANK, (c + 1) * BANK)
+            z = psum.tile([P, BANK], F32, name="z", tag="bank%d" % bank)
             nc.tensor.matmul_mx(
-                out=acc[:],
-                lhsT=wa_w[:, 2 * P * b : 2 * P * (b + 1)].bitcast(FP4X4),
-                lhsT_scale=wa_s[:, P * b : P * (b + 1)],
-                rhs=codes[:, slots(h)].bitcast(FP8X4),
-                rhs_scale=scales[:, slots(h)],
+                out=z[:],
+                lhsT=ws_w[:, 2 * P * b : 2 * P * (b + 1)].bitcast(FP4X4),
+                lhsT_scale=ws_s[:, P * b : P * (b + 1)],
+                rhs=xs_w[:, cols].bitcast(FP8X4),
+                rhs_scale=xs_s[:, cols],
                 start=True,
                 stop=True,
             )
-            tag = "u0" if (b, h) == (1, 0) else "d%d%s" % (b, h)
-            d = keep.tile([P, width], F32, name="d", tag=tag, align_bytes=64)
-            nc.scalar.activation(d[:], acc[:], RELU)
-            nc.vector.tensor_copy(placed[b][:].indirect(entries(tok_list, h)), d[:])
+            return z
 
         def finish(b, banks):
             for c in range(T // BANK):
                 cols = slice(c * BANK, (c + 1) * BANK)
-                z = psum.tile([P, BANK], F32, name="z", tag="bank%d" % banks[c])
-                nc.tensor.matmul_mx(
-                    out=z[:],
-                    lhsT=ws_w[:, 2 * P * b : 2 * P * (b + 1)].bitcast(FP4X4),
-                    lhsT_scale=ws_s[:, P * b : P * (b + 1)],
-                    rhs=xs_w[:, cols].bitcast(FP8X4),
-                    rhs_scale=xs_s[:, cols],
-                    start=True,
-                    stop=True,
-                )
+                z = shared(b, c, banks[c])
                 y = keep.tile([P, BANK], F32, name="y%d%d" % (b, c))
                 if b == BLOCKS - 1:
                     nc.vector.tensor_tensor(y[:], z[:], placed[b][:, cols], ADD)
@@ -143,17 +142,19 @@ def tile_moe_expert_reads_token_and_context_kernel(
                     nc.gpsimd.tensor_tensor(y[:], zs[:], placed[b][:, cols], ADD)
                 nc.sync.dma_start(out[b * P : (b + 1) * P, cols], y[:])
 
-        for t, h in ((0, 0), (0, 1), (1, 0), (1, 1), (2, 0), (3, 0), (2, 1)):
-            gather(t, h)
+        for t in range(PACK):
+            for h in range(2):
+                gather(t, h)
         quantise(0)
-        gather(3, 1)
-        expert(0, 0, 0)
+        placed[2] = keep.tile([P, T], F32, name="placed2", tag="u0", align_bytes=64)
+        nc.vector.memset(placed[2][:].bitcast(I32), 0)
         quantise(1)
-        expert(1, 0, 1)
-        expert(0, 1, 2)
-        expert(1, 1, 3)
-        expert(2, None, 4)
-        expert(3, None, 5)
+        expert(0, 0, HALF, 0)
+        expert(1, 0, HALF, 1)
+        expert(0, HALF, J, 2)
+        expert(1, HALF, J, 3)
+        expert(2, 0, J, 4)
+        expert(3, 0, J, 5)
         finish(0, (2, 3))
         finish(1, (4, 5))
         finish(2, (2, 3))

from contextlib import ExitStack

import concourse.mybir as mybir

K, T, V, J, L, N = 512, 1024, 512, 512, 512, 512
FLOPS = 2 * K * N * J + 2 * L * N * T

F32 = mybir.dt.float32
BF16 = mybir.dt.bfloat16
I32 = mybir.dt.int32
U32 = mybir.dt.uint32
U16 = mybir.dt.uint16
U8 = mybir.dt.uint8
FP8X4 = mybir.dt.float8_e4m3fn_x4
FP4X4 = mybir.dt.float4_e2m1fn_x4
ADD = mybir.AluOpType.add
COPY = mybir.ActivationFunctionType.Copy
RELU = mybir.ActivationFunctionType.Relu

P = 128
PACK = 4
HALF = J // 2
BANK = 512
BLOCKS = N // P


def tile_moe_expert_reads_token_and_context_kernel(
    tc, xf, cx, fk, wa_words, wa_scales, xs_words, xs_scales, ws_words, ws_scales, offs, offs2, out
):
    nc = tc.nc
    with ExitStack() as ctx:
        keep = ctx.enter_context(tc.tile_pool(name="keep", bufs=1))
        psum = ctx.enter_context(tc.psum_pool(name="psum", bufs=1))

        tok_list = keep.tile([P, J // 16], U16, name="tok_list")
        ctx_list = keep.tile([P, J // 16], U16, name="ctx_list")
        factor = keep.tile([P, PACK], F32, name="factor")
        tokens = [keep.tile([P, T], F32, name="tokens%d" % t) for t in range(PACK)]
        contexts = [keep.tile([P, V], F32, name="contexts%d" % t) for t in range(PACK)]
        wa_w = keep.tile([P, 2 * N], U8, name="wa_w", align_bytes=64)
        ws_w = keep.tile([P, 2 * N], U8, name="ws_w", align_bytes=64)
        xs_w = keep.tile([P, T], U32, name="xs_w", align_bytes=64)
        wa_s = keep.tile([P, N], U8, name="wa_s", align_bytes=64)
        ws_s = keep.tile([P, N], U8, name="ws_s", align_bytes=64)
        xs_s = keep.tile([P, T], U8, name="xs_s", align_bytes=64)
        placed = {b: keep.tile([P, T], F32, name="placed%d" % b) for b in (0, 1, 3)}

        for plane in (wa_s, ws_s, xs_s):
            nc.gpsimd.memset(plane[:].bitcast(I32), 0)
        for b in (0, 1, 3):
            nc.vector.memset(placed[b][:].bitcast(I32), 0)

        xf_rows = xf.rearrange("(p t) c -> t p c", t=PACK)
        cx_rows = cx.rearrange("(p t) c -> t p c", t=PACK)
        nc.sync.dma_start(ctx_list[:], offs2)
        nc.sync.dma_start(contexts[0][:], cx_rows[0])
        nc.sync.dma_start(tok_list[:], offs)
        nc.sync.dma_start(tokens[0][:], xf_rows[0])
        nc.sync.dma_start(factor[:], fk.rearrange("(p t) o -> p (t o)", t=PACK))
        for t in range(1, PACK):
            nc.sync.dma_start(contexts[t][:], cx_rows[t])
            nc.sync.dma_start(tokens[t][:], xf_rows[t])

        def load_scales(plane, rows):
            for q in range(4):
                nc.sync.dma_start(
                    plane[32 * q : 32 * q + 4, :].bitcast(I32), rows[0, 4 * q : 4 * q + 4, :].bitcast(I32)
                )

        nc.sync.dma_start(wa_w[:].bitcast(I32), wa_words[0].bitcast(I32))
        load_scales(wa_s, wa_scales)
        nc.sync.dma_start(ws_w[:].bitcast(I32), ws_words[0].bitcast(I32))
        nc.sync.dma_start(xs_w[:].bitcast(I32), xs_words[0].rearrange("p c r -> p (c r)").bitcast(I32))
        load_scales(ws_s, ws_scales)
        load_scales(xs_s, xs_scales)

        def slots(h):
            return slice(0, J) if h is None else slice(h * HALF, (h + 1) * HALF)

        def entries(lst, h):
            return lst[:, slots(h).start // 16 : slots(h).stop // 16]

        u = [keep.tile([P, HALF, PACK], BF16, name="u%d" % h, tag="u%d" % h, align_bytes=64) for h in range(2)]
        codes = keep.tile([P, J], U32, name="codes", align_bytes=64)
        scales = keep.tile([P, J], U8, name="scales", align_bytes=64)

        def gather(t, h):
            picked = keep.tile([P, HALF], F32, name="picked", tag="picked%d%d" % (t, h))
            summed = keep.tile([P, HALF], F32, name="summed%d%d" % (t, h))
            nc.vector.tensor_copy(picked[:], contexts[t][:].indirect(entries(ctx_list, h)))
            nc.vector.tensor_tensor(summed[:], tokens[t][:].indirect(entries(tok_list, h)), picked[:], ADD)
            nc.scalar.activation(u[h][:, :, t], summed[:], COPY, scale=factor[:, t : t + 1])

        def quantise(h):
            nc.vector.quantize_mx(
                out=codes[:, slots(h)].bitcast(FP8X4),
                scales=scales[:, slots(h)],
                in_=u[h][:].rearrange("p j t -> p (j t)"),
            )

        def expert(b, lo, hi, bank):
            acc = psum.tile([P, hi - lo], F32, name="expert_acc", tag="bank%d" % bank)
            cuts = (lo, HALF, hi) if 0 < lo < HALF < hi else (lo, hi)
            for first, last in zip(cuts, cuts[1:]):
                nc.tensor.matmul_mx(
                    out=acc[:, first - lo : last - lo],
                    lhsT=wa_w[:, 2 * P * b : 2 * P * (b + 1)].bitcast(FP4X4),
                    lhsT_scale=wa_s[:, P * b : P * (b + 1)],
                    rhs=codes[:, first:last].bitcast(FP8X4),
                    rhs_scale=scales[:, first:last],
                    start=True,
                    stop=True,
                )
            d = keep.tile([P, hi - lo], F32, name="d%d_%d" % (b, lo))
            nc.scalar.activation(d[:], acc[:], RELU)
            nc.vector.tensor_copy(placed[b][:].indirect(tok_list[:, lo // 16 : hi // 16]), d[:])

        def shared(b, c, bank):
            cols = slice(c * BANK, (c + 1) * BANK)
            z = psum.tile([P, BANK], F32, name="z", tag="bank%d" % bank)
            nc.tensor.matmul_mx(
                out=z[:],
                lhsT=ws_w[:, 2 * P * b : 2 * P * (b + 1)].bitcast(FP4X4),
                lhsT_scale=ws_s[:, P * b : P * (b + 1)],
                rhs=xs_w[:, cols].bitcast(FP8X4),
                rhs_scale=xs_s[:, cols],
                start=True,
                stop=True,
            )
            return z

        def finish(b, banks):
            for c in range(T // BANK):
                cols = slice(c * BANK, (c + 1) * BANK)
                z = shared(b, c, banks[c])
                y = keep.tile([P, BANK], F32, name="y%d%d" % (b, c))
                if b == BLOCKS - 1:
                    nc.vector.tensor_tensor(y[:], z[:], placed[b][:, cols], ADD)
                else:
                    zs = keep.tile([P, BANK], F32, name="zs%d%d" % (b, c))
                    nc.scalar.copy(zs[:], z[:])
                    nc.gpsimd.tensor_tensor(y[:], zs[:], placed[b][:, cols], ADD)
                nc.sync.dma_start(out[b * P : (b + 1) * P, cols], y[:])

        for t in range(PACK):
            for h in range(2):
                gather(t, h)
        quantise(0)
        placed[2] = keep.tile([P, T], F32, name="placed2", tag="u0", align_bytes=64)
        nc.vector.memset(placed[2][:].bitcast(I32), 0)
        quantise(1)
        expert(0, 0, HALF, 0)
        expert(1, 0, HALF, 1)
        expert(0, HALF, J, 2)
        expert(1, HALF, J, 3)
        expert(2, 0, J, 4)
        expert(3, 0, J, 5)
        finish(0, (2, 3))
        finish(1, (4, 5))
        finish(2, (2, 3))
        finish(3, (6, 7))
